import numpy as np, ml_dtypes
CORES = [8,136,40,168]
N = 4
import mx_ref
KO = 3
F = np.float32(0.6)
OWN = [1,1,1,1]
BF = ml_dtypes.bfloat16
def tile(rs):
    return np.stack(rs, axis=2).reshape(128, -1).astype(BF)
def pick(b):
    s = np.zeros((128, 128, 4), np.float32)
    s[np.arange(128), np.arange(128), b] = 1.0
    return mx_ref.quantize(s.reshape(128, 512).astype(BF))
def pk(c, s, i=0):
    return (np.ascontiguousarray(c[:, 512 * i:512 * i + 512]), mx_ref.live(s[:, 128 * i:128 * i + 128]))
def inputs(rng, e, E):
    def f(*shape):
        v = (rng.standard_normal(shape, dtype=np.float32) * np.exp2(rng.integers(-2, 3, shape[:-1] + (1,)))).astype(BF)
        return mx_ref.spread((v.astype(np.float32) * np.exp2(rng.integers(-E, E + 1, shape[:-2] + (1, 1))).astype(np.float32)).astype(BF), rng, e)
    def packed(k):
        c = np.zeros((N, 128, k * 512), np.uint8); s = np.zeros((N, 128, k * 128), np.uint8)
        for r in range(N):
            for i in range(k):
                a, b = mx_ref.quantize(f(128, 512)); c[r][:, 512 * i:512 * i + 512] = a; s[r][:, 128 * i:128 * i + 128] = mx_ref.plane(b, rng)
        return c, s
    d = {}
    d["kc"], d["ks"] = packed(KO)
    d["q"] = f(N, 128, 512)
    return d
def setup_inputs(rng):
    return inputs(rng, 0, 0)
def setup_inputs_blocks(rng):
    return inputs(rng, 4, 0)
def setup_inputs_wide(rng):
    return inputs(rng, 0, 8)
def reference(kc, ks, q):
    S = [pick(t) for t in range(4)]
    anew = lambda p, i: mx_ref.quantize(tile([mx_ref.matmul(S[t], pk(kc[p], ks[p], i)) * F for t in range(4)]))
    y = np.full((N, 128, 1536), np.nan, np.float32)
    for o in range(N):
        if OWN[o] != o: continue
        qq = mx_ref.quantize(q[o])
        M = [pk(kc[o], ks[o], i) for i in range(KO)] + [anew(p, i) for p in range(N) if p != o and OWN[p] == o for i in range(KO)]
        y[o][:, :128 * len(M)] = np.concatenate([mx_ref.matmul(qq, m) for m in M], axis=1)
    return {"y": y}

@@ -1,0 +1,153 @@
+from concourse.mybir import dt, AluOpType, ActivationFunctionType
+
+W = 128
+KO = 3
+SENDS = [[0], [1, 2]]
+NP = 3
+FACTOR = 0.6
+BANK = 512
+BANKS = 8
+
+SCRATCH = {
+    "kcod": ("sbuf", [128, KO * W], "float8_e4m3fn_x4"),
+    "kpln": ("sbuf", [128, KO * W], "uint8"),
+    "strip": ("sbuf", [128, 4 * W + 8], "bfloat16"),
+    "scod": ("sbuf", [128, 4 * W], "float8_e4m3fn_x4"),
+    "spln": ("sbuf", [128, 4 * W], "uint8"),
+    "anew": ("sbuf", [128, 4 * KO * W], "bfloat16"),
+    "ncod": ("sbuf", [128, KO * W], "float8_e4m3fn_x4"),
+    "npln": ("sbuf", [128, KO * W], "uint8"),
+    "qbf": ("sbuf", [128, 4 * W], "bfloat16"),
+    "qcod": ("sbuf", [128, W], "float8_e4m3fn_x4"),
+    "qpln": ("sbuf", [128, W], "uint8"),
+    "lcod": ("sbuf", [128, NP * KO * W], "float8_e4m3fn_x4"),
+    "lpln": ("sbuf", [128, NP * KO * W], "uint8"),
+    "ysb": ("sbuf", [128, (NP + 1) * KO * W], "float32"),
+    "ps": ("psum", [128, BANK * BANKS], "float32"),
+}
+SEMAPHORES = (["ld0", "ld1", "ldp", "ldq", "zero", "diag", "sq", "qq", "mm", "cv", "cs", "nq", "sent", "sty", "sta"]
+              + ["arr%d_%d" % (p, k) for p in range(NP) for k in range(len(SENDS))])
+
+
+def bank(T, k, n):
+    k = k % BANKS
+    return T.ps[:, BANK * k:BANK * k + n]
+
+
+def producer(g, core, T, topo, dst, slot):
+    v, s, t = g.vector, g.scalar, g.tensor
+    sem = T.sem
+    U8 = dt.uint8
+    g.sync.dma_start(T.kcod[:, 0:W].bitcast(U8), T.kc[:, 0:4 * W]).then_inc(sem.ld0, 16)
+    s.dma_start(T.kpln[:, 0:KO * W], T.ks[:, 0:KO * W]).then_inc(sem.ldp, 16)
+    g.sync.dma_start(T.kcod[:, W:KO * W].bitcast(U8), T.kc[:, 4 * W:4 * KO * W]).then_inc(sem.ld1, 16)
+
+    v.memset(T.strip[:], 0.0).then_inc(sem.zero, 1)
+    g.wait_ge(sem.zero, 1)
+    g.affine_select(T.strip[:, 4:4 + 4 * W:4], T.strip[:, 4:4 + 4 * W:4], [[-1, W]], AluOpType.not_equal, 1.0, 0, 1).then_inc(sem.diag, 1)
+    v.wait_ge(sem.diag, 1)
+    for b in range(4):
+        v.quantize_mx(T.scod[:, W * b:W * (b + 1)], T.spln[:, W * b:W * (b + 1)], T.strip[:, 4 - b:4 - b + 4 * W]).then_inc(sem.sq, 1)
+
+    t.wait_ge(sem.ld0, 16)
+    t.wait_ge(sem.ldp, 16)
+    for i in range(KO):
+        if i == 1:
+            t.wait_ge(sem.ld1, 16)
+        if i >= 2:
+            t.wait_ge(sem.cv, 2 * (i - 1))
+            t.wait_ge(sem.cs, 2 * (i - 1))
+        for b in range(4):
+            if i == 0:
+                t.wait_ge(sem.sq, b + 1)
+            t.matmul_mx(bank(T, 4 * i + b, W), T.scod[:, W * b:W * (b + 1)], T.spln[:, W * b:W * (b + 1)],
+                        T.kcod[:, W * i:W * (i + 1)], T.kpln[:, W * i:W * (i + 1)], True, True).then_inc(sem.mm, 1)
+
+    for i in range(KO):
+        for b in range(4):
+            out = T.anew[:, 4 * W * i + b:4 * W * (i + 1):4]
+            if b % 2 == 0:
+                s.wait_ge(sem.mm, 4 * i + b + 1)
+                s.activation(out, bank(T, 4 * i + b, W), ActivationFunctionType.Copy, scale=FACTOR).then_inc(sem.cs, 1)
+            else:
+                v.wait_ge(sem.mm, 4 * i + b + 1)
+                v.tensor_scalar(out, bank(T, 4 * i + b, W), FACTOR, None, AluOpType.mult).then_inc(sem.cv, 1)
+        v.wait_ge(sem.cs, 2 * (i + 1))
+        v.wait_ge(sem.cv, 2 * (i + 1))
+        v.quantize_mx(T.ncod[:, W * i:W * (i + 1)], T.npln[:, W * i:W * (i + 1)],
+                      T.anew[:, 4 * W * i:4 * W * (i + 1)]).then_inc(sem.nq, 1)
+
+    rid, pid = topo.addr(dst, core)
+    mask = topo.mask(core, dst)
+    engines = bin(mask).count("1")
+    base = slot * KO * W
+    for k, tiles in enumerate(SENDS):
+        a, b = W * tiles[0], W * (tiles[-1] + 1)
+        g.wait_ge(sem.nq, tiles[-1] + 1)
+        arr = sem["arr%d_%d" % (slot, k)]
+        g.remote_dma(out_ap=T.lcod[:, base + a:base + b].bitcast(U8), in_ap=T.ncod[:, a:b].bitcast(U8), remote_sem=arr,
+                     local_sem=sem.sent, pid=pid, routing_id=rid, dma_engine_mask=mask)
+        g.remote_dma(out_ap=T.lpln[:, base + a:base + b], in_ap=T.npln[:, a:b], remote_sem=arr,
+                     local_sem=sem.sent, pid=pid, routing_id=rid, dma_engine_mask=mask)
+    g.wait_ge(sem.sent, 2 * len(SENDS) * engines)
+
+
+def consumer(g, core, T, topo, senders):
+    v, s, t = g.vector, g.scalar, g.tensor
+    sem = T.sem
+    g.sync.dma_start(T.qbf[:], T.q[:]).then_inc(sem.ldq, 16)
+    s.dma_start(T.kpln[:, 0:KO * W], T.ks[:, 0:KO * W]).then_inc(sem.ldp, 16)
+    g.sync.dma_start(T.kcod[:, 0:KO * W].bitcast(dt.uint8), T.kc[:, 0:4 * KO * W]).then_inc(sem.ld0, 16)
+    v.wait_ge(sem.ldq, 16)
+    v.quantize_mx(T.qcod[:], T.qpln[:], T.qbf[:]).then_inc(sem.qq, 1)
+
+    units = [(0, KO * W, T.kcod[:, 0:KO * W], T.kpln[:, 0:KO * W], [(sem.qq, 1), (sem.ld0, 16), (sem.ldp, 16)])]
+    stores = [(0, 0)]
+    for k, tiles in enumerate(SENDS):
+        for slot, src in enumerate(senders):
+            engines = bin(topo.mask(src, core)).count("1")
+            stores.append((len(units), len(units) + len(tiles) - 1))
+            for i in tiles:
+                a = W * (slot * KO + i)
+                wait = [(sem["arr%d_%d" % (slot, k)], 2 * engines)] if i == tiles[0] else []
+                units.append((KO * W + a, W, T.lcod[:, a:a + W], T.lpln[:, a:a + W], wait))
+
+    def emptied(q, u):
+        q.wait_ge(sem.cv if u % 2 == 0 else sem.cs, u // 2 + 1)
+
+    for u, (y0, n, cod, pln, wait) in enumerate(units):
+        for w in wait:
+            t.wait_ge(w[0], w[1])
+        if u >= BANKS:
+            emptied(t, u - BANKS)
+        t.matmul_mx(bank(T, u, n), T.qcod[:], T.qpln[:], cod, pln, True, True).then_inc(sem.mm, 1)
+        if u % 2 == 0:
+            v.wait_ge(sem.mm, u + 1)
+            v.tensor_copy(T.ysb[:, y0:y0 + n], bank(T, u, n)).then_inc(sem.cv, 1)
+        else:
+            s.wait_ge(sem.mm, u + 1)
+            s.activation(T.ysb[:, y0:y0 + n], bank(T, u, n), ActivationFunctionType.Copy).then_inc(sem.cs, 1)
+
+    for j, (u0, u1) in enumerate(stores):
+        last = j == len(stores) - 1
+        q, done = (s, sem.sta) if last else (g.sync, sem.sty)
+        for u in range(u0, u1 + 1):
+            emptied(q, u)
+        y0, y1 = units[u0][0], units[u1][0] + units[u1][1]
+        q.dma_start(T.y[:, y0:y1], T.ysb[:, y0:y1]).then_inc(done, 16)
+    g.sync.wait_ge(sem.sty, 16 * (len(stores) - 1))
+    s.wait_ge(sem.sta, 16)
+    v.wait_ge(sem.cv, (len(units) + 1) // 2)
+
+
+def rank_program(g, core, T, topo):
+    rank = T.rank_of(core)
+    if rank is None:
+        return
+    own = T.tables["OWN"]
+    o = own[rank]
+    senders = [p for p in range(len(own)) if p != o and own[p] == o]
+    if rank == o:
+        consumer(g, core, T, topo, [T.cores[p] for p in senders])
+    else:
+        producer(g, core, T, topo, T.cores[o], senders.index(rank))

@@ -2,8 +2,10 @@ from concourse.mybir import dt, AluOpType, ActivationFunctionType
 
 W = 128
 KO = 3
-SENDS = [[0], [1, 2]]
+RELAYED = [0]
+ORDER = [1, 2, 0]
 NP = 3
+WORLD = 256
 FACTOR = 0.6
 BANK = 512
 BANKS = 8
@@ -25,8 +27,29 @@ SCRATCH = {
     "ysb": ("sbuf", [128, (NP + 1) * KO * W], "float32"),
     "ps": ("psum", [128, BANK * BANKS], "float32"),
 }
-SEMAPHORES = (["ld0", "ld1", "ldp", "ldq", "zero", "diag", "sq", "qq", "mm", "cv", "cs", "nq", "sent", "sty", "sta"]
-              + ["arr%d_%d" % (p, k) for p in range(NP) for k in range(len(SENDS))])
+SEMAPHORES = (["ld0", "ld1", "ldp", "ldq", "zero", "diag", "sq", "qq", "mm", "cv", "cs", "nq", "sent", "sty", "sta", "rc", "rp"]
+              + ["arr%d_%d" % (p, i) for p in range(NP) for i in range(KO)])
+U8 = dt.uint8
+
+
+def count(mask):
+    return bin(mask).count("1")
+
+
+def relay_of(topo, src, dst):
+    for c in range(WORLD):
+        if (topo.host(c), topo.chip(c)) == (topo.host(src), topo.chip(src)) and topo.die(c) != topo.die(src) and topo.may_write(c, dst):
+            return c
+
+
+def onchip(topo, src, relay, dst):
+    return topo.mask(src, relay) & ~topo.mask(src, dst)
+
+
+def direct(topo, src, dst):
+    every = topo.mask(src, dst)
+    bits = [e for e in range(every.bit_length()) if every >> e & 1]
+    return sum(1 << e for e in bits[::2])
 
 
 def bank(T, k, n):
@@ -37,7 +60,6 @@ def bank(T, k, n):
 def producer(g, core, T, topo, dst, slot):
     v, s, t = g.vector, g.scalar, g.tensor
     sem = T.sem
-    U8 = dt.uint8
     g.sync.dma_start(T.kcod[:, 0:W].bitcast(U8), T.kc[:, 0:4 * W]).then_inc(sem.ld0, 16)
     s.dma_start(T.kpln[:, 0:KO * W], T.ks[:, 0:KO * W]).then_inc(sem.ldp, 16)
     g.sync.dma_start(T.kcod[:, W:KO * W].bitcast(U8), T.kc[:, 4 * W:4 * KO * W]).then_inc(sem.ld1, 16)
@@ -77,19 +99,40 @@ def producer(g, core, T, topo, dst, slot):
         v.quantize_mx(T.ncod[:, W * i:W * (i + 1)], T.npln[:, W * i:W * (i + 1)],
                       T.anew[:, 4 * W * i:4 * W * (i + 1)]).then_inc(sem.nq, 1)
 
+    relay = relay_of(topo, core, dst)
+    sent = 0
+    for i in range(KO):
+        a, b = W * i, W * (i + 1)
+        g.wait_ge(sem.nq, i + 1)
+        if i in RELAYED:
+            rid, pid = topo.addr(relay, core)
+            mask = onchip(topo, core, relay, dst)
+            outs = (T.npln[:, a:b], sem.rp), (T.ncod[:, a:b].bitcast(U8), sem.rc)
+        else:
+            rid, pid = topo.addr(dst, core)
+            mask = direct(topo, core, dst)
+            la, lb, arr = W * KO * slot + a, W * KO * slot + b, sem["arr%d_%d" % (slot, i)]
+            outs = (T.lpln[:, la:lb], arr), (T.lcod[:, la:lb].bitcast(U8), arr)
+        for (out, arr), src in zip(outs, (T.npln[:, a:b], T.ncod[:, a:b].bitcast(U8))):
+            g.remote_dma(out_ap=out, in_ap=src, remote_sem=arr, local_sem=sem.sent, pid=pid, routing_id=rid, dma_engine_mask=mask)
+            sent += count(mask)
+    g.wait_ge(sem.sent, sent)
+
+
+def relay_program(g, core, T, topo, src, dst, slot):
     rid, pid = topo.addr(dst, core)
     mask = topo.mask(core, dst)
-    engines = bin(mask).count("1")
-    base = slot * KO * W
-    for k, tiles in enumerate(SENDS):
-        a, b = W * tiles[0], W * (tiles[-1] + 1)
-        g.wait_ge(sem.nq, tiles[-1] + 1)
-        arr = sem["arr%d_%d" % (slot, k)]
-        g.remote_dma(out_ap=T.lcod[:, base + a:base + b].bitcast(U8), in_ap=T.ncod[:, a:b].bitcast(U8), remote_sem=arr,
-                     local_sem=sem.sent, pid=pid, routing_id=rid, dma_engine_mask=mask)
-        g.remote_dma(out_ap=T.lpln[:, base + a:base + b], in_ap=T.npln[:, a:b], remote_sem=arr,
-                     local_sem=sem.sent, pid=pid, routing_id=rid, dma_engine_mask=mask)
-    g.wait_ge(sem.sent, 2 * len(SENDS) * engines)
+    came = count(onchip(topo, src, core, dst))
+    for n, i in enumerate(RELAYED):
+        a, b = W * i, W * (i + 1)
+        la, lb, arr = W * KO * slot + a, W * KO * slot + b, T.sem["arr%d_%d" % (slot, i)]
+        g.wait_ge(T.sem.rp, came * (n + 1))
+        g.remote_dma(out_ap=T.lpln[:, la:lb], in_ap=T.npln[:, a:b], remote_sem=arr, local_sem=T.sem.sent,
+                     pid=pid, routing_id=rid, dma_engine_mask=mask)
+        g.wait_ge(T.sem.rc, came * (n + 1))
+        g.remote_dma(out_ap=T.lcod[:, la:lb].bitcast(U8), in_ap=T.ncod[:, a:b].bitcast(U8), remote_sem=arr, local_sem=T.sem.sent,
+                     pid=pid, routing_id=rid, dma_engine_mask=mask)
+    g.wait_ge(T.sem.sent, 2 * len(RELAYED) * count(mask))
 
 
 def consumer(g, core, T, topo, senders):
@@ -97,20 +140,16 @@ def consumer(g, core, T, topo, senders):
     sem = T.sem
     g.sync.dma_start(T.qbf[:], T.q[:]).then_inc(sem.ldq, 16)
     s.dma_start(T.kpln[:, 0:KO * W], T.ks[:, 0:KO * W]).then_inc(sem.ldp, 16)
-    g.sync.dma_start(T.kcod[:, 0:KO * W].bitcast(dt.uint8), T.kc[:, 0:4 * KO * W]).then_inc(sem.ld0, 16)
+    g.sync.dma_start(T.kcod[:, 0:KO * W].bitcast(U8), T.kc[:, 0:4 * KO * W]).then_inc(sem.ld0, 16)
     v.wait_ge(sem.ldq, 16)
     v.quantize_mx(T.qcod[:], T.qpln[:], T.qbf[:]).then_inc(sem.qq, 1)
 
     units = [(0, KO * W, T.kcod[:, 0:KO * W], T.kpln[:, 0:KO * W], [(sem.qq, 1), (sem.ld0, 16), (sem.ldp, 16)])]
-    stores = [(0, 0)]
-    for k, tiles in enumerate(SENDS):
+    for i in ORDER:
         for slot, src in enumerate(senders):
-            engines = bin(topo.mask(src, core)).count("1")
-            stores.append((len(units), len(units) + len(tiles) - 1))
-            for i in tiles:
-                a = W * (slot * KO + i)
-                wait = [(sem["arr%d_%d" % (slot, k)], 2 * engines)] if i == tiles[0] else []
-                units.append((KO * W + a, W, T.lcod[:, a:a + W], T.lpln[:, a:a + W], wait))
+            last = topo.mask(relay_of(topo, src, core), core) if i in RELAYED else direct(topo, src, core)
+            a = W * (slot * KO + i)
+            units.append((KO * W + a, W, T.lcod[:, a:a + W], T.lpln[:, a:a + W], [(sem["arr%d_%d" % (slot, i)], 2 * count(last))]))
 
     def emptied(q, u):
         q.wait_ge(sem.cv if u % 2 == 0 else sem.cs, u // 2 + 1)
@@ -127,27 +166,22 @@ def consumer(g, core, T, topo, senders):
         else:
             s.wait_ge(sem.mm, u + 1)
             s.activation(T.ysb[:, y0:y0 + n], bank(T, u, n), ActivationFunctionType.Copy).then_inc(sem.cs, 1)
-
-    for j, (u0, u1) in enumerate(stores):
-        last = j == len(stores) - 1
-        q, done = (s, sem.sta) if last else (g.sync, sem.sty)
-        for u in range(u0, u1 + 1):
-            emptied(q, u)
-        y0, y1 = units[u0][0], units[u1][0] + units[u1][1]
-        q.dma_start(T.y[:, y0:y1], T.ysb[:, y0:y1]).then_inc(done, 16)
-    g.sync.wait_ge(sem.sty, 16 * (len(stores) - 1))
+        q, done = (s, sem.sta) if u == len(units) - 1 else (g.sync, sem.sty)
+        emptied(q, u)
+        q.dma_start(T.y[:, y0:y0 + n], T.ysb[:, y0:y0 + n]).then_inc(done, 16)
+    g.sync.wait_ge(sem.sty, 16 * (len(units) - 1))
     s.wait_ge(sem.sta, 16)
-    v.wait_ge(sem.cv, (len(units) + 1) // 2)
 
 
 def rank_program(g, core, T, topo):
-    rank = T.rank_of(core)
-    if rank is None:
-        return
     own = T.tables["OWN"]
-    o = own[rank]
-    senders = [p for p in range(len(own)) if p != o and own[p] == o]
-    if rank == o:
-        consumer(g, core, T, topo, [T.cores[p] for p in senders])
-    else:
-        producer(g, core, T, topo, T.cores[o], senders.index(rank))
+    for o in sorted(set(own)):
+        dst = T.cores[o]
+        senders = [T.cores[p] for p in range(len(own)) if p != o and own[p] == o]
+        if core == dst:
+            consumer(g, core, T, topo, senders)
+        for slot, src in enumerate(senders):
+            if core == src:
+                producer(g, core, T, topo, dst, slot)
+            elif core == relay_of(topo, src, dst):
+                relay_program(g, core, T, topo, src, dst, slot)

from concourse.mybir import dt, AluOpType, ActivationFunctionType

W = 128
KO = 3
RELAYED = [0]
ORDER = [1, 2, 0]
NP = 3
WORLD = 256
FACTOR = 0.6
BANK = 512
BANKS = 8

SCRATCH = {
    "kcod": ("sbuf", [128, KO * W], "float8_e4m3fn_x4"),
    "kpln": ("sbuf", [128, KO * W], "uint8"),
    "strip": ("sbuf", [128, 4 * W + 8], "bfloat16"),
    "scod": ("sbuf", [128, 4 * W], "float8_e4m3fn_x4"),
    "spln": ("sbuf", [128, 4 * W], "uint8"),
    "anew": ("sbuf", [128, 4 * KO * W], "bfloat16"),
    "ncod": ("sbuf", [128, KO * W], "float8_e4m3fn_x4"),
    "npln": ("sbuf", [128, KO * W], "uint8"),
    "qbf": ("sbuf", [128, 4 * W], "bfloat16"),
    "qcod": ("sbuf", [128, W], "float8_e4m3fn_x4"),
    "qpln": ("sbuf", [128, W], "uint8"),
    "lcod": ("sbuf", [128, NP * KO * W], "float8_e4m3fn_x4"),
    "lpln": ("sbuf", [128, NP * KO * W], "uint8"),
    "ysb": ("sbuf", [128, (NP + 1) * KO * W], "float32"),
    "ps": ("psum", [128, BANK * BANKS], "float32"),
}
SEMAPHORES = (["ld0", "ld1", "ldp", "ldq", "zero", "diag", "sq", "qq", "mm", "cv", "cs", "nq", "sent", "sty", "sta", "rc", "rp"]
              + ["arr%d_%d" % (p, i) for p in range(NP) for i in range(KO)])
U8 = dt.uint8


def count(mask):
    return bin(mask).count("1")


def relay_of(topo, src, dst):
    for c in range(WORLD):
        if (topo.host(c), topo.chip(c)) == (topo.host(src), topo.chip(src)) and topo.die(c) != topo.die(src) and topo.may_write(c, dst):
            return c


def onchip(topo, src, relay, dst):
    return topo.mask(src, relay) & ~topo.mask(src, dst)


def direct(topo, src, dst):
    every = topo.mask(src, dst)
    bits = [e for e in range(every.bit_length()) if every >> e & 1]
    return sum(1 << e for e in bits[::2])


def bank(T, k, n):
    k = k % BANKS
    return T.ps[:, BANK * k:BANK * k + n]


def producer(g, core, T, topo, dst, slot):
    v, s, t = g.vector, g.scalar, g.tensor
    sem = T.sem
    g.sync.dma_start(T.kcod[:, 0:W].bitcast(U8), T.kc[:, 0:4 * W]).then_inc(sem.ld0, 16)
    s.dma_start(T.kpln[:, 0:KO * W], T.ks[:, 0:KO * W]).then_inc(sem.ldp, 16)
    g.sync.dma_start(T.kcod[:, W:KO * W].bitcast(U8), T.kc[:, 4 * W:4 * KO * W]).then_inc(sem.ld1, 16)

    v.memset(T.strip[:], 0.0).then_inc(sem.zero, 1)
    g.wait_ge(sem.zero, 1)
    g.affine_select(T.strip[:, 4:4 + 4 * W:4], T.strip[:, 4:4 + 4 * W:4], [[-1, W]], AluOpType.not_equal, 1.0, 0, 1).then_inc(sem.diag, 1)
    v.wait_ge(sem.diag, 1)
    for b in range(4):
        v.quantize_mx(T.scod[:, W * b:W * (b + 1)], T.spln[:, W * b:W * (b + 1)], T.strip[:, 4 - b:4 - b + 4 * W]).then_inc(sem.sq, 1)

    t.wait_ge(sem.ld0, 16)
    t.wait_ge(sem.ldp, 16)
    for i in range(KO):
        if i == 1:
            t.wait_ge(sem.ld1, 16)
        if i >= 2:
            t.wait_ge(sem.cv, 2 * (i - 1))
            t.wait_ge(sem.cs, 2 * (i - 1))
        for b in range(4):
            if i == 0:
                t.wait_ge(sem.sq, b + 1)
            t.matmul_mx(bank(T, 4 * i + b, W), T.scod[:, W * b:W * (b + 1)], T.spln[:, W * b:W * (b + 1)],
                        T.kcod[:, W * i:W * (i + 1)], T.kpln[:, W * i:W * (i + 1)], True, True).then_inc(sem.mm, 1)

    for i in range(KO):
        for b in range(4):
            out = T.anew[:, 4 * W * i + b:4 * W * (i + 1):4]
            if b % 2 == 0:
                s.wait_ge(sem.mm, 4 * i + b + 1)
                s.activation(out, bank(T, 4 * i + b, W), ActivationFunctionType.Copy, scale=FACTOR).then_inc(sem.cs, 1)
            else:
                v.wait_ge(sem.mm, 4 * i + b + 1)
                v.tensor_scalar(out, bank(T, 4 * i + b, W), FACTOR, None, AluOpType.mult).then_inc(sem.cv, 1)
        v.wait_ge(sem.cs, 2 * (i + 1))
        v.wait_ge(sem.cv, 2 * (i + 1))
        v.quantize_mx(T.ncod[:, W * i:W * (i + 1)], T.npln[:, W * i:W * (i + 1)],
                      T.anew[:, 4 * W * i:4 * W * (i + 1)]).then_inc(sem.nq, 1)

    relay = relay_of(topo, core, dst)
    sent = 0
    for i in range(KO):
        a, b = W * i, W * (i + 1)
        g.wait_ge(sem.nq, i + 1)
        if i in RELAYED:
            rid, pid = topo.addr(relay, core)
            mask = onchip(topo, core, relay, dst)
            outs = (T.npln[:, a:b], sem.rp), (T.ncod[:, a:b].bitcast(U8), sem.rc)
        else:
            rid, pid = topo.addr(dst, core)
            mask = direct(topo, core, dst)
            la, lb, arr = W * KO * slot + a, W * KO * slot + b, sem["arr%d_%d" % (slot, i)]
            outs = (T.lpln[:, la:lb], arr), (T.lcod[:, la:lb].bitcast(U8), arr)
        for (out, arr), src in zip(outs, (T.npln[:, a:b], T.ncod[:, a:b].bitcast(U8))):
            g.remote_dma(out_ap=out, in_ap=src, remote_sem=arr, local_sem=sem.sent, pid=pid, routing_id=rid, dma_engine_mask=mask)
            sent += count(mask)
    g.wait_ge(sem.sent, sent)


def relay_program(g, core, T, topo, src, dst, slot):
    rid, pid = topo.addr(dst, core)
    mask = topo.mask(core, dst)
    came = count(onchip(topo, src, core, dst))
    for n, i in enumerate(RELAYED):
        a, b = W * i, W * (i + 1)
        la, lb, arr = W * KO * slot + a, W * KO * slot + b, T.sem["arr%d_%d" % (slot, i)]
        g.wait_ge(T.sem.rp, came * (n + 1))
        g.remote_dma(out_ap=T.lpln[:, la:lb], in_ap=T.npln[:, a:b], remote_sem=arr, local_sem=T.sem.sent,
                     pid=pid, routing_id=rid, dma_engine_mask=mask)
        g.wait_ge(T.sem.rc, came * (n + 1))
        g.remote_dma(out_ap=T.lcod[:, la:lb].bitcast(U8), in_ap=T.ncod[:, a:b].bitcast(U8), remote_sem=arr, local_sem=T.sem.sent,
                     pid=pid, routing_id=rid, dma_engine_mask=mask)
    g.wait_ge(T.sem.sent, 2 * len(RELAYED) * count(mask))


def consumer(g, core, T, topo, senders):
    v, s, t = g.vector, g.scalar, g.tensor
    sem = T.sem
    g.sync.dma_start(T.qbf[:], T.q[:]).then_inc(sem.ldq, 16)
    s.dma_start(T.kpln[:, 0:KO * W], T.ks[:, 0:KO * W]).then_inc(sem.ldp, 16)
    g.sync.dma_start(T.kcod[:, 0:KO * W].bitcast(U8), T.kc[:, 0:4 * KO * W]).then_inc(sem.ld0, 16)
    v.wait_ge(sem.ldq, 16)
    v.quantize_mx(T.qcod[:], T.qpln[:], T.qbf[:]).then_inc(sem.qq, 1)

    units = [(0, KO * W, T.kcod[:, 0:KO * W], T.kpln[:, 0:KO * W], [(sem.qq, 1), (sem.ld0, 16), (sem.ldp, 16)])]
    for i in ORDER:
        for slot, src in enumerate(senders):
            last = topo.mask(relay_of(topo, src, core), core) if i in RELAYED else direct(topo, src, core)
            a = W * (slot * KO + i)
            units.append((KO * W + a, W, T.lcod[:, a:a + W], T.lpln[:, a:a + W], [(sem["arr%d_%d" % (slot, i)], 2 * count(last))]))

    def emptied(q, u):
        q.wait_ge(sem.cv if u % 2 == 0 else sem.cs, u // 2 + 1)

    for u, (y0, n, cod, pln, wait) in enumerate(units):
        for w in wait:
            t.wait_ge(w[0], w[1])
        if u >= BANKS:
            emptied(t, u - BANKS)
        t.matmul_mx(bank(T, u, n), T.qcod[:], T.qpln[:], cod, pln, True, True).then_inc(sem.mm, 1)
        if u % 2 == 0:
            v.wait_ge(sem.mm, u + 1)
            v.tensor_copy(T.ysb[:, y0:y0 + n], bank(T, u, n)).then_inc(sem.cv, 1)
        else:
            s.wait_ge(sem.mm, u + 1)
            s.activation(T.ysb[:, y0:y0 + n], bank(T, u, n), ActivationFunctionType.Copy).then_inc(sem.cs, 1)
        q, done = (s, sem.sta) if u == len(units) - 1 else (g.sync, sem.sty)
        emptied(q, u)
        q.dma_start(T.y[:, y0:y0 + n], T.ysb[:, y0:y0 + n]).then_inc(done, 16)
    g.sync.wait_ge(sem.sty, 16 * (len(units) - 1))
    s.wait_ge(sem.sta, 16)


def rank_program(g, core, T, topo):
    own = T.tables["OWN"]
    for o in sorted(set(own)):
        dst = T.cores[o]
        senders = [T.cores[p] for p in range(len(own)) if p != o and own[p] == o]
        if core == dst:
            consumer(g, core, T, topo, senders)
        for slot, src in enumerate(senders):
            if core == src:
                producer(g, core, T, topo, dst, slot)
            elif core == relay_of(topo, src, dst):
                relay_program(g, core, T, topo, src, dst, slot)
